import numpy as np
import ml_dtypes


def mxq(x, axis, fmt="e4m3"):
    dtype, down = {"e4m3": (ml_dtypes.float8_e4m3fn, 7), "e5m2": (ml_dtypes.float8_e5m2, 14)}[fmt]
    v = np.moveaxis(np.asarray(x, np.float32).astype(ml_dtypes.bfloat16).astype(np.float64), axis, -1)
    blocks = v.reshape(v.shape[:-1] + (-1, 32))
    amax = np.abs(blocks).max(-1, keepdims=True)
    byte = np.maximum(np.where(amax > 0, np.frexp(amax)[1] - 1 + 127, 0) - down, 1)
    scale = np.exp2(byte - 127.0)
    codes = (blocks / scale).astype(np.float32).astype(dtype).astype(np.float64)
    return np.moveaxis((codes * scale).reshape(v.shape), -1, axis)


WIDE = False


def mx_kscale(k):
    if not WIDE:
        return np.ones(k)
    levels = np.array([10, -10, 5, -5, 0])
    if k % 512:
        return np.exp2(np.random.permutation(np.resize(levels, k // 32))).repeat(32)
    a = np.empty((k // 512, 16))
    for p in range(k // 512):
        a[p, :8] = np.random.permutation(np.resize(levels, 8))
        for g in range(8):
            far = levels[np.abs(levels - a[p, g]) >= 10]
            a[p, g + 8] = far[np.random.randint(len(far))]
    return np.exp2(a.ravel()).repeat(32)


def f64(x):
    return np.asarray(x).astype(np.float64)


def striped(idx):
    return np.tile(np.asarray(idx).reshape(-1, 16).T, (8, 1)).astype(np.uint16)


def unstriped(offs):
    return offs[:16].T.reshape(-1).astype(np.int64)


E2M1 = np.array([0.0, 0.5, 1.0, 1.5, 2.0, 3.0, 4.0, 6.0, -0.0, -0.5, -1.0, -1.5, -2.0, -3.0, -4.0, -6.0])


def pack_weight(w, fmt):
    k, n = w.shape
    w = f64(np.asarray(w, np.float32).astype(ml_dtypes.bfloat16)).reshape(k // 32, 32, n)
    amax = np.abs(w).max(1)
    if fmt == "e4m3":
        byte = np.frexp(amax)[1] - 1 + 127 - 7
    else:
        mant, ex = np.frexp(amax / 6.0)
        byte = np.where(mant > 0.5, ex, ex - 1) + 127
    byte = np.clip(np.where(amax > 0, byte, 1), 1, 254)
    scaled = (w * np.exp2(127.0 - byte)[:, None, :]).reshape(k, n).astype(np.float32)
    by_word = np.ascontiguousarray(scaled.reshape(k // 512, 128, 4, n).transpose(0, 1, 3, 2))
    if fmt == "e4m3":
        words = by_word.astype(ml_dtypes.float8_e4m3fn).view(np.uint8)
    else:
        c = by_word.astype(ml_dtypes.float4_e2m1fn).view(np.uint8) & 0xF
        words = (c[..., 0::2] | (c[..., 1::2] << 4)).reshape(k // 512, 128, 2 * n)
    return np.ascontiguousarray(words), np.ascontiguousarray(byte.astype(np.uint8).reshape(k // 512, 16, n))


def unpack_weight(words, scales, fmt):
    g, _, n = scales.shape
    words = np.ascontiguousarray(words).reshape(g, 128, n, -1)
    if fmt == "e4m3":
        vals = words.view(ml_dtypes.float8_e4m3fn).astype(np.float64)
    else:
        nib = np.empty((g, 128, n, 4), np.uint8)
        nib[..., 0::2] = words & 0xF
        nib[..., 1::2] = words >> 4
        vals = E2M1[nib]
    vals = vals * np.repeat(np.exp2(scales.astype(np.float64) - 127.0), 8, axis=1)[..., None]
    return vals.transpose(0, 1, 3, 2).reshape(g * 512, n)


def bf(x):
    return np.asarray(x, np.float32).astype(ml_dtypes.bfloat16)


def planes(Y):
    r, m = Y.shape
    b = f64(bf(Y)).reshape(r // 32, 32, m)
    amax = np.abs(b).max(1)
    byte = np.clip(np.where(amax > 0, np.frexp(amax)[1] - 1 + 127 - 7, 1), 1, 254)
    codes = (b * np.exp2(127.0 - byte)[:, None, :]).reshape(r, m).astype(np.float32).astype(ml_dtypes.float8_e4m3fn).view(np.uint8)
    words = codes.reshape(r // 512, 128, 4, m).transpose(0, 1, 3, 2)
    return np.ascontiguousarray(words), np.ascontiguousarray(byte.astype(np.uint8).reshape(r // 512, 16, m))


K, R, F, T, J, M = 512, 512, 512, 2048, 512, 256


def setup_inputs():
    n = np.random.standard_normal
    idx = np.random.permutation(T)[:J]
    idx2 = np.random.permutation(J)[:M]
    idx3 = np.random.permutation(J)[:M]
    fk = mx_kscale(K)
    fr = mx_kscale(R)
    dtabp = pack_weight(n((K, T)) / fk[:, None], "e4m3")
    tabp = pack_weight(n((K, T)) / fk[:, None], "e4m3")
    return {
        "dtab_words": dtabp[0],
        "dtab_scales": dtabp[1],
        "tab_words": tabp[0],
        "tab_scales": tabp[1],
        "w1": (n((K, R)) * 1 / np.sqrt(K) * fk[:, None]).astype(np.float32),
        "reserve": (np.random.uniform(0.3, 1.5, (R, 1))).astype(np.float32),
        "rs": (np.random.uniform(0.5, 2.0, (R, 1)) * fr[:, None]).astype(np.float32),
        "wor": (n((R, F)) * 1 / np.sqrt(R) / fr[:, None]).astype(np.float32),
        "res": (n((F, M)) * 0.5).astype(np.float32),
        "offs": striped(idx),
        "offs2": striped(idx2),
        "offs3": striped(idx3),
    }


def reference(dtab_words, dtab_scales, tab_words, tab_scales, w1, reserve, rs, wor, res, offs, offs2, offs3):
    idx = unstriped(offs)
    idx2 = unstriped(offs2)
    idx3 = unstriped(offs3)
    dtabu = unpack_weight(dtab_words, dtab_scales, "e4m3")
    tabu = unpack_weight(tab_words, tab_scales, "e4m3")
    w1q = mxq(f64(w1), 0, "e4m3")
    tabidxg = tabu[:, idx]
    a = w1q.T @ tabidxg
    dtabidxg = dtabu[:, idx]
    ta = w1q.T @ dtabidxg
    h1 = np.exp(a)
    th1 = ta * h1
    tu1 = (th1[:, idx2] - (th1[:, idx2] + th1[:, idx3]) * h1[:, idx2] / (h1[:, idx2] + h1[:, idx3] + f64(reserve))) / (h1[:, idx2] + h1[:, idx3] + f64(reserve))
    fo1 = tu1 * f64(rs)
    worq = mxq(f64(wor), 0, "e4m3")
    fo1q = mxq(fo1, 0, "e4m3")
    yo = worq.T @ fo1q
    y = yo + f64(res)
    words, scales = planes(y)
    return y, words, scales

@@ -1,0 +1,232 @@
+from contextlib import ExitStack
+
+import concourse.mybir as mybir
+from concourse.masks import make_identity
+
+K, R, F, T, J, M = 512, 512, 512, 2048, 512, 256
+FLOPS = 2 * K * R * J * 2 + 2 * R * F * M
+
+F32 = mybir.dt.float32
+BF16 = mybir.dt.bfloat16
+I32 = mybir.dt.int32
+U32 = mybir.dt.uint32
+U16 = mybir.dt.uint16
+U8 = mybir.dt.uint8
+FP8X4 = mybir.dt.float8_e4m3fn_x4
+ACT = mybir.ActivationFunctionType
+ALU = mybir.AluOpType
+
+P = 128
+PACK = 4
+QUADS = 4
+HALVES = 2
+MH = M // HALVES
+
+
+def tile_attend_tratiopairs_o_pl_kernel(
+    tc, dtab_words, dtab_scales, tab_words, tab_scales, w1, reserve, rs, wor, res, offs, offs2, offs3, out_0, out_1, out_2
+):
+    nc = tc.nc
+    with ExitStack() as ctx:
+        keep = ctx.enter_context(tc.tile_pool(name="keep", bufs=1))
+        psum = ctx.enter_context(tc.psum_pool(name="psum", bufs=1))
+
+        def sb(name, shape, dtype):
+            return keep.tile(shape, dtype, name=name, align_bytes=64)
+
+        def bank(name, number, shape):
+            return psum.tile(shape, F32, name=name, tag="bank%d" % number)
+
+        def load_scale_rows(queues, plane, rows):
+            for q, queue in enumerate(queues):
+                queue.dma_start(plane[32 * q : 32 * q + 4, :].bitcast(I32), rows[0, 4 * q : 4 * q + 4, :].bitcast(I32))
+
+        def load_words(tile, words):
+            nc.sync.dma_start(tile[:].bitcast(I32), words[0].rearrange("p n t -> p (n t)").bitcast(I32))
+
+        slots = sb("slots", [P, J // 16], U16)
+        firsts = sb("firsts", [P, M // 16], U16)
+        seconds = sb("seconds", [P, M // 16], U16)
+        tab_w = sb("tab_w", [P, T], U32)
+        dtab_w = sb("dtab_w", [P, T], U32)
+        tab_s = sb("tab_s", [P, T], U8)
+        dtab_s = sb("dtab_s", [P, T], U8)
+        w1_raw = sb("w1_raw", [P, PACK, R], F32)
+        reserve_sb = sb("reserve_sb", [P, PACK], F32)
+        rs_sb = sb("rs_sb", [P, PACK], F32)
+
+        nc.gpsimd.memset(tab_s[:].bitcast(I32), 0)
+        nc.vector.memset(dtab_s[:].bitcast(I32), 0)
+
+        nc.sync.dma_start(slots[:], offs)
+        nc.sync.dma_start(w1_raw[:], w1.rearrange("(p j) c -> p j c", j=PACK))
+        load_scale_rows((nc.scalar, nc.scalar, nc.gpsimd, nc.gpsimd), tab_s, tab_scales)
+        load_words(tab_w, tab_words)
+        load_words(dtab_w, dtab_words)
+        load_scale_rows((nc.gpsimd,) * QUADS, dtab_s, dtab_scales)
+        nc.sync.dma_start(firsts[:], offs2)
+        nc.sync.dma_start(seconds[:], offs3)
+        nc.gpsimd.dma_start(reserve_sb[:], reserve.rearrange("(p t) o -> p (t o)", t=PACK))
+        nc.gpsimd.dma_start(rs_sb[:], rs.rearrange("(p t) o -> p (t o)", t=PACK))
+
+        ident = sb("ident", [P, P], F32)
+        make_identity(nc, ident[:])
+
+        reserve_rs = sb("reserve_rs", [P, PACK], F32)
+        nc.gpsimd.tensor_tensor(reserve_rs[:], reserve_sb[:], rs_sb[:], ALU.mult)
+        minus_rs = sb("minus_rs", [P, PACK], F32)
+        nc.gpsimd.tensor_scalar(minus_rs[:], rs_sb[:], -1.0, 0.0, ALU.mult, ALU.add)
+
+        tab_gw = sb("tab_gw", [P, J], U32)
+        tab_gs = sb("tab_gs", [P, J], U8)
+        nc.vector.tensor_copy(tab_gs[:], tab_s[:].indirect(slots[:]))
+
+        w1_bf = sb("w1_bf", [P, PACK, P, PACK], BF16)
+        dealt = w1_bf[:].rearrange("p t m j -> p m j t")
+        natural = w1_raw[:].rearrange("p j (m t) -> p m j t", t=PACK)
+        nc.scalar.activation(dealt[:, : P // 2], natural[:, : P // 2], ACT.Copy)
+        nc.vector.tensor_copy(dealt[:, P // 2 :], natural[:, P // 2 :])
+        wor_raw = sb("w1_raw", [P, PACK, F], F32)
+        nc.sync.dma_start(wor_raw[:], wor.rearrange("(p j) c -> p j c", j=PACK))
+        w1_codes = [sb("w1_codes%d" % t, [P, P], U32) for t in range(PACK)]
+        w1_scales = [sb("w1_scales%d" % t, [P, P], U8) for t in range(PACK)]
+        for t in range(PACK):
+            nc.vector.quantize_mx(
+                out=w1_codes[t][:].bitcast(FP8X4), scales=w1_scales[t][:], in_=w1_bf[:, t, :, :].rearrange("p m j -> p (m j)")
+            )
+
+        nc.vector.tensor_copy(tab_gw[:], tab_w[:].indirect(slots[:]))
+        res_sb = sb("tab_w", [P, PACK, M], F32)
+        nc.sync.dma_start(res_sb[:], res.rearrange("(p t) m -> p t m", t=PACK))
+
+        dtab_gw = sb("dtab_gw", [P, J], U32)
+        dtab_gs = sb("w1_bf", [P, J], U8)
+        nc.vector.tensor_copy(dtab_gs[:], dtab_s[:].indirect(slots[:]))
+        nc.vector.tensor_copy(dtab_gw[:], dtab_w[:].indirect(slots[:]))
+
+        def first_layer(acc, t, words, scales):
+            nc.tensor.matmul_mx(
+                out=acc[:],
+                lhsT=w1_codes[t][:].bitcast(FP8X4),
+                lhsT_scale=w1_scales[t][:],
+                rhs=words[:].bitcast(FP8X4),
+                rhs_scale=scales[:],
+                start=True,
+                stop=True,
+            )
+
+        h1 = [sb("h1_%d" % t, [P, J], F32) for t in range(PACK)]
+        for t in range(PACK):
+            a = bank("a%d" % t, t, [P, J])
+            first_layer(a, t, tab_gw, tab_gs)
+            nc.scalar.activation(h1[t][:], a[:], ACT.Exp)
+        ta = [bank("ta%d" % t, PACK + t, [P, J]) for t in range(PACK)]
+        for t in range(PACK):
+            first_layer(ta[t], t, dtab_gw, dtab_gs)
+
+        h_first = [sb("h_first%d" % t, [P, M], F32) for t in range(PACK)]
+        h_second = [sb("h_second%d" % t, [P, M], F32) for t in range(PACK)]
+        own = [sb("own%d" % t, [P, M], F32) for t in range(PACK)]
+        rest = [sb("rest%d" % t, [P, M], F32) for t in range(PACK)]
+        den_t = [bank("den_t%d" % u, u, [P, PACK, P]) for u in range(HALVES)]
+        for t in range(PACK):
+            nc.vector.tensor_copy(h_first[t][:], h1[t][:].indirect(firsts[:]))
+            nc.vector.tensor_copy(h_second[t][:], h1[t][:].indirect(seconds[:]))
+            for u in range(HALVES):
+                cols = slice(u * MH, (u + 1) * MH)
+                terms = (reserve_sb[:, t : t + 1].to_broadcast([P, P]), h_first[t][:, cols], h_second[t][:, cols])
+                for n, term in enumerate(terms):
+                    nc.tensor.matmul(
+                        den_t[u][:, t, :], lhsT=term, rhs=ident[:], is_transpose=True, start=(n == 0), stop=(n == len(terms) - 1)
+                    )
+            nc.scalar.activation(own[t][:], h_first[t][:], ACT.Copy, scale=minus_rs[:, t : t + 1])
+            nc.scalar.activation(
+                rest[t][:], h_second[t][:], ACT.Identity, scale=rs_sb[:, t : t + 1], bias=reserve_rs[:, t : t + 1]
+            )
+
+        abs_t = sb("abs_t", [P, HALVES, PACK * P], F32)
+        for u in range(HALVES):
+            nc.scalar.activation(abs_t[:, u, :], den_t[u][:].rearrange("p t r -> p (t r)"), ACT.Abs)
+        log_t = sb("log_t", [P, HALVES, PACK * P], F32)
+        nc.scalar.activation(log_t[:], abs_t[:], ACT.Ln)
+        inv_sq_t = [sb("inv_sq_t%d" % u, [P, 2, P, 2], F32) for u in range(HALVES)]
+        for u in range(HALVES):
+            nc.scalar.activation(inv_sq_t[u][:], log_t[:, u, :].rearrange("p (w e r) -> p w r e", w=2, e=2), ACT.Exp, scale=-2.0)
+
+        th1 = [sb("th1_%d" % t, [P, J], F32) for t in range(PACK)]
+        for t in range(PACK):
+            nc.vector.tensor_tensor(th1[t][:], ta[t][:], h1[t][:], ALU.mult)
+
+        wor_bf = sb("wor_bf", [P, PACK, P, PACK], BF16)
+        for q in range(4):
+            nc.scalar.copy(
+                wor_bf[:, :, q * 32 : (q + 1) * 32, :].rearrange("p t m j -> p m j t"),
+                wor_raw[:, :, q * P : (q + 1) * P].rearrange("p j (m t) -> p m j t", t=PACK),
+            )
+        wor_codes = sb("wor_codes", [P, F], U32)
+        wor_scales = sb("wor_scales", [P, F], U8)
+        nc.vector.quantize_mx(
+            out=wor_codes[:].bitcast(FP8X4), scales=wor_scales[:], in_=wor_bf[:].rearrange("p t m j -> p (t m j)")
+        )
+
+        numer_t = [bank("numer_t%d" % u, HALVES + u, [P, PACK, P]) for u in range(HALVES)]
+        for t in range(PACK):
+            gain = sb("gain%d" % t, [P, M], F32)
+            loss = sb("loss%d" % t, [P, M], F32)
+            nc.vector.tensor_tensor(gain[:], th1[t][:].indirect(firsts[:]), rest[t][:], ALU.mult)
+            nc.vector.tensor_tensor(loss[:], th1[t][:].indirect(seconds[:]), own[t][:], ALU.mult)
+            for u in range(HALVES):
+                cols = slice(u * MH, (u + 1) * MH)
+                for n, term in enumerate((gain, loss)):
+                    nc.tensor.matmul(
+                        numer_t[u][:, t, :], lhsT=term[:, cols], rhs=ident[:], is_transpose=True, start=(n == 0), stop=(n == 1)
+                    )
+
+        y_bf = sb("y_bf", [P, M, PACK], BF16)
+        out_rows = out_0.rearrange("(p t) m -> p t m", t=PACK)
+        fo_codes, fo_scales = [], []
+        for u in range(HALVES):
+            fo_t = sb("fo_t%d" % u, [P, 2, P, 2], BF16)
+            nc.vector.tensor_tensor(
+                fo_t[:], numer_t[u][:].rearrange("p (w e) r -> p w r e", e=2), inv_sq_t[u][:], ALU.mult
+            )
+            fo_words = fo_t[:].rearrange("p w r e -> p (w r e)").bitcast(F32)
+            turned = bank("turned%d" % u, u, [P, 2, MH])
+            for w in range(2):
+                nc.tensor.transpose(turned[:, w, :], fo_words[:, w * P : (w + 1) * P], ident[:])
+            fo_bf = sb("fo_bf%d" % u, [P, MH, PACK], BF16)
+            nc.scalar.copy(
+                fo_bf[:].rearrange("p m t -> p (m t)").bitcast(F32).rearrange("p (m w) -> p m w", w=2),
+                turned[:].rearrange("p w m -> p m w"),
+            )
+            fo_codes.append(sb("fo_codes%d" % u, [P, MH], U32))
+            fo_scales.append(sb("fo_scales%d" % u, [P, MH], U8))
+            nc.vector.quantize_mx(
+                out=fo_codes[u][:].bitcast(FP8X4), scales=fo_scales[u][:], in_=fo_bf[:].rearrange("p m t -> p (m t)")
+            )
+        for u in range(HALVES):
+            cols = slice(u * MH, (u + 1) * MH)
+            yo = bank("yo%d" % u, PACK + u, [P, PACK, MH])
+            for t in range(PACK):
+                nc.tensor.matmul_mx(
+                    out=yo[:, t, :],
+                    lhsT=wor_codes[:, t * P : (t + 1) * P].bitcast(FP8X4),
+                    lhsT_scale=wor_scales[:, t * P : (t + 1) * P],
+                    rhs=fo_codes[u][:].bitcast(FP8X4),
+                    rhs_scale=fo_scales[u][:],
+                    start=True,
+                    stop=True,
+                )
+            y = sb("y%d" % u, [P, PACK, MH], F32)
+            nc.vector.tensor_tensor(y[:], yo[:], res_sb[:, :, cols], ALU.add)
+            nc.sync.dma_start(out_rows[:, :, cols], y[:])
+            nc.scalar.copy(
+                y_bf[:, cols, :].rearrange("p (a i) t -> p a t i", i=4), y[:].rearrange("p t (a i) -> p a t i", i=4)
+            )
+
+        y_codes = sb("y_codes", [P, M], U32)
+        y_scales = sb("y_scales", [P, M], U8)
+        nc.vector.quantize_mx(out=y_codes[:].bitcast(FP8X4), scales=y_scales[:], in_=y_bf[:].rearrange("p m t -> p (m t)"))
+        nc.sync.dma_start(out_1[0].rearrange("p m t -> p (m t)").bitcast(I32), y_codes[:].bitcast(I32))
+        for q, queue in enumerate((nc.scalar, nc.sync, nc.scalar, nc.sync)):
+            queue.dma_start(out_2[0, 4 * q : 4 * q + 4, :].bitcast(I32), y_scales[32 * q : 32 * q + 4, :].bitcast(I32))

@@ -38,8 +38,8 @@ def tile_attend_tratiopairs_o_pl_kernel(
             return psum.tile(shape, F32, name=name, tag="bank%d" % number)
 
         def load_scale_rows(queues, plane, rows):
-            for q, queue in enumerate(queues):
-                queue.dma_start(plane[32 * q : 32 * q + 4, :].bitcast(I32), rows[0, 4 * q : 4 * q + 4, :].bitcast(I32))
+            for i, queue in enumerate(queues):
+                queue.dma_start(plane[i:P:32, :].bitcast(I32), rows[0, i:16:4, :].bitcast(I32))
 
         def load_words(tile, words):
             nc.sync.dma_start(tile[:].bitcast(I32), words[0].rearrange("p n t -> p (n t)").bitcast(I32))
@@ -51,19 +51,21 @@ def tile_attend_tratiopairs_o_pl_kernel(
         dtab_w = sb("dtab_w", [P, T], U32)
         tab_s = sb("tab_s", [P, T], U8)
         dtab_s = sb("dtab_s", [P, T], U8)
-        w1_raw = sb("w1_raw", [P, PACK, R], F32)
+        w1_raw = [sb("w1_raw%d" % h, [P, PACK, R // 2], F32) for h in range(2)]
         reserve_sb = sb("reserve_sb", [P, PACK], F32)
         rs_sb = sb("rs_sb", [P, PACK], F32)
 
         nc.gpsimd.memset(tab_s[:].bitcast(I32), 0)
-        nc.vector.memset(dtab_s[:].bitcast(I32), 0)
+        nc.gpsimd.memset(dtab_s[:].bitcast(I32), 0)
 
         nc.sync.dma_start(slots[:], offs)
-        nc.sync.dma_start(w1_raw[:], w1.rearrange("(p j) c -> p j c", j=PACK))
-        load_scale_rows((nc.scalar, nc.scalar, nc.gpsimd, nc.gpsimd), tab_s, tab_scales)
         load_words(tab_w, tab_words)
+        load_scale_rows((nc.sync,) * 4, tab_s, tab_scales)
+        w1_rows = w1.rearrange("(p j) c -> p j c", j=PACK)
+        for h in range(2):
+            nc.sync.dma_start(w1_raw[h][:], w1_rows[:, :, h * (R // 2) : (h + 1) * (R // 2)])
+        load_scale_rows((nc.sync,) * 4, dtab_s, dtab_scales)
         load_words(dtab_w, dtab_words)
-        load_scale_rows((nc.gpsimd,) * QUADS, dtab_s, dtab_scales)
         nc.sync.dma_start(firsts[:], offs2)
         nc.sync.dma_start(seconds[:], offs3)
         nc.gpsimd.dma_start(reserve_sb[:], reserve.rearrange("(p t) o -> p (t o)", t=PACK))
@@ -79,36 +81,38 @@ def tile_attend_tratiopairs_o_pl_kernel(
 
         tab_gw = sb("tab_gw", [P, J], U32)
         tab_gs = sb("tab_gs", [P, J], U8)
+        dtab_gw = sb("dtab_gw", [P, J], U32)
+        dtab_gs = sb("dtab_gs", [P, J], U8)
+        nc.vector.tensor_copy(tab_gw[:], tab_w[:].indirect(slots[:]))
         nc.vector.tensor_copy(tab_gs[:], tab_s[:].indirect(slots[:]))
 
         w1_bf = sb("w1_bf", [P, PACK, P, PACK], BF16)
         dealt = w1_bf[:].rearrange("p t m j -> p m j t")
-        natural = w1_raw[:].rearrange("p j (m t) -> p m j t", t=PACK)
-        nc.scalar.activation(dealt[:, : P // 2], natural[:, : P // 2], ACT.Copy)
-        nc.vector.tensor_copy(dealt[:, P // 2 :], natural[:, P // 2 :])
-        wor_raw = sb("w1_raw", [P, PACK, F], F32)
-        nc.sync.dma_start(wor_raw[:], wor.rearrange("(p j) c -> p j c", j=PACK))
-        w1_codes = [sb("w1_codes%d" % t, [P, P], U32) for t in range(PACK)]
-        w1_scales = [sb("w1_scales%d" % t, [P, P], U8) for t in range(PACK)]
-        for t in range(PACK):
+        natural = [w1_raw[h][:].rearrange("p j (m t) -> p m j t", t=PACK) for h in range(2)]
+        nc.scalar.activation(dealt[:, :64], natural[0], ACT.Copy)
+        nc.scalar.activation(dealt[:, 64:88], natural[1][:, :24], ACT.Copy)
+        nc.vector.tensor_copy(dealt[:, 88:], natural[1][:, 24:])
+        w1_codes = [sb("w1_codes%d" % h, [P, 2 * P], U32) for h in range(2)]
+        w1_scales = [sb("w1_scales%d" % h, [P, 2 * P], U8) for h in range(2)]
+        for h in range(2):
             nc.vector.quantize_mx(
-                out=w1_codes[t][:].bitcast(FP8X4), scales=w1_scales[t][:], in_=w1_bf[:, t, :, :].rearrange("p m j -> p (m j)")
+                out=w1_codes[h][:].bitcast(FP8X4),
+                scales=w1_scales[h][:],
+                in_=w1_bf[:, 2 * h : 2 * h + 2, :, :].rearrange("p t m j -> p (t m j)"),
             )
-
-        nc.vector.tensor_copy(tab_gw[:], tab_w[:].indirect(slots[:]))
-        res_sb = sb("tab_w", [P, PACK, M], F32)
-        nc.sync.dma_start(res_sb[:], res.rearrange("(p t) m -> p t m", t=PACK))
-
-        dtab_gw = sb("dtab_gw", [P, J], U32)
-        dtab_gs = sb("w1_bf", [P, J], U8)
         nc.vector.tensor_copy(dtab_gs[:], dtab_s[:].indirect(slots[:]))
         nc.vector.tensor_copy(dtab_gw[:], dtab_w[:].indirect(slots[:]))
+
+        wor_raw = sb("tab_w", [P, PACK, F], F32)
+        nc.sync.dma_start(wor_raw[:], wor.rearrange("(p j) c -> p j c", j=PACK))
+        res_sb = sb("w1_raw0", [P, PACK, M], F32)
+        nc.sync.dma_start(res_sb[:], res.rearrange("(p t) m -> p t m", t=PACK))
 
         def first_layer(acc, t, words, scales):
             nc.tensor.matmul_mx(
                 out=acc[:],
-                lhsT=w1_codes[t][:].bitcast(FP8X4),
-                lhsT_scale=w1_scales[t][:],
+                lhsT=w1_codes[t // 2][:, (t % 2) * P : (t % 2 + 1) * P].bitcast(FP8X4),
+                lhsT_scale=w1_scales[t // 2][:, (t % 2) * P : (t % 2 + 1) * P],
                 rhs=words[:].bitcast(FP8X4),
                 rhs_scale=scales[:],
                 start=True,
@@ -144,14 +148,13 @@ def tile_attend_tratiopairs_o_pl_kernel(
                 rest[t][:], h_second[t][:], ACT.Identity, scale=rs_sb[:, t : t + 1], bias=reserve_rs[:, t : t + 1]
             )
 
-        abs_t = sb("abs_t", [P, HALVES, PACK * P], F32)
-        for u in range(HALVES):
-            nc.scalar.activation(abs_t[:, u, :], den_t[u][:].rearrange("p t r -> p (t r)"), ACT.Abs)
-        log_t = sb("log_t", [P, HALVES, PACK * P], F32)
-        nc.scalar.activation(log_t[:], abs_t[:], ACT.Ln)
         inv_sq_t = [sb("inv_sq_t%d" % u, [P, 2, P, 2], F32) for u in range(HALVES)]
         for u in range(HALVES):
-            nc.scalar.activation(inv_sq_t[u][:], log_t[:, u, :].rearrange("p (w e r) -> p w r e", w=2, e=2), ACT.Exp, scale=-2.0)
+            root_t = sb("root_t%d" % u, [P, PACK * P], F32)
+            inv_t = sb("inv_t%d" % u, [P, PACK * P], F32)
+            nc.scalar.activation(root_t[:], den_t[u][:].rearrange("p t r -> p (t r)"), ACT.Abs_reciprocal_sqrt)
+            nc.scalar.activation(inv_t[:], root_t[:], ACT.Square)
+            nc.scalar.activation(inv_sq_t[u][:], inv_t[:].rearrange("p (w e r) -> p w r e", w=2, e=2), ACT.Square)
 
         th1 = [sb("th1_%d" % t, [P, J], F32) for t in range(PACK)]
         for t in range(PACK):

@@ -52,11 +52,11 @@ def tile_attend_tratiopairs_o_pl_kernel(
         tab_s = sb("tab_s", [P, T], U8)
         dtab_s = sb("dtab_s", [P, T], U8)
         w1_raw = [sb("w1_raw%d" % h, [P, PACK, R // 2], F32) for h in range(2)]
-        reserve_sb = sb("reserve_sb", [P, PACK], F32)
-        rs_sb = sb("rs_sb", [P, PACK], F32)
+        vectors = sb("vectors", [P, P], F32)
 
         nc.gpsimd.memset(tab_s[:].bitcast(I32), 0)
         nc.gpsimd.memset(dtab_s[:].bitcast(I32), 0)
+        nc.gpsimd.memset(vectors[:], 0.0)
 
         nc.sync.dma_start(slots[:], offs)
         load_words(tab_w, tab_words)
@@ -68,16 +68,11 @@ def tile_attend_tratiopairs_o_pl_kernel(
         load_words(dtab_w, dtab_words)
         nc.sync.dma_start(firsts[:], offs2)
         nc.sync.dma_start(seconds[:], offs3)
-        nc.gpsimd.dma_start(reserve_sb[:], reserve.rearrange("(p t) o -> p (t o)", t=PACK))
-        nc.gpsimd.dma_start(rs_sb[:], rs.rearrange("(p t) o -> p (t o)", t=PACK))
+        nc.sync.dma_start(vectors[0:PACK, :], reserve.rearrange("(t p) o -> t (p o)", t=PACK))
+        nc.sync.dma_start(vectors[PACK : 2 * PACK, :], rs.rearrange("(t p) o -> t (p o)", t=PACK))
 
         ident = sb("ident", [P, P], F32)
         make_identity(nc, ident[:])
-
-        reserve_rs = sb("reserve_rs", [P, PACK], F32)
-        nc.gpsimd.tensor_tensor(reserve_rs[:], reserve_sb[:], rs_sb[:], ALU.mult)
-        minus_rs = sb("minus_rs", [P, PACK], F32)
-        nc.gpsimd.tensor_scalar(minus_rs[:], rs_sb[:], -1.0, 0.0, ALU.mult, ALU.add)
 
         tab_gw = sb("tab_gw", [P, J], U32)
         tab_gs = sb("tab_gs", [P, J], U8)
@@ -86,19 +81,15 @@ def tile_attend_tratiopairs_o_pl_kernel(
         nc.vector.tensor_copy(tab_gw[:], tab_w[:].indirect(slots[:]))
         nc.vector.tensor_copy(tab_gs[:], tab_s[:].indirect(slots[:]))
 
-        w1_bf = sb("w1_bf", [P, PACK, P, PACK], BF16)
-        dealt = w1_bf[:].rearrange("p t m j -> p m j t")
-        natural = [w1_raw[h][:].rearrange("p j (m t) -> p m j t", t=PACK) for h in range(2)]
-        nc.scalar.activation(dealt[:, :64], natural[0], ACT.Copy)
-        nc.scalar.activation(dealt[:, 64:88], natural[1][:, :24], ACT.Copy)
-        nc.vector.tensor_copy(dealt[:, 88:], natural[1][:, 24:])
+        w1_bf = [sb("w1_bf%d" % h, [P, R // 2, PACK], BF16) for h in range(2)]
         w1_codes = [sb("w1_codes%d" % h, [P, 2 * P], U32) for h in range(2)]
         w1_scales = [sb("w1_scales%d" % h, [P, 2 * P], U8) for h in range(2)]
         for h in range(2):
+            nc.scalar.activation(
+                w1_bf[h][:].rearrange("p (a i) j -> p a j i", i=4), w1_raw[h][:].rearrange("p j (a i) -> p a j i", i=4), ACT.Copy
+            )
             nc.vector.quantize_mx(
-                out=w1_codes[h][:].bitcast(FP8X4),
-                scales=w1_scales[h][:],
-                in_=w1_bf[:, 2 * h : 2 * h + 2, :, :].rearrange("p t m j -> p (t m j)"),
+                out=w1_codes[h][:].bitcast(FP8X4), scales=w1_scales[h][:], in_=w1_bf[h][:].rearrange("p c j -> p (c j)")
             )
         nc.vector.tensor_copy(dtab_gs[:], dtab_s[:].indirect(slots[:]))
         nc.vector.tensor_copy(dtab_gw[:], dtab_w[:].indirect(slots[:]))
@@ -128,6 +119,18 @@ def tile_attend_tratiopairs_o_pl_kernel(
         for t in range(PACK):
             first_layer(ta[t], t, dtab_gw, dtab_gs)
 
+        vectors_t = bank("vectors_t", PACK - 1, [P, P])
+        nc.tensor.transpose(vectors_t[:], vectors[:], ident[:])
+        reserve_sb = sb("reserve_sb", [P, PACK], F32)
+        rs_sb = sb("rs_sb", [P, PACK], F32)
+        minus_rs = sb("minus_rs", [P, PACK], F32)
+        reserve_rs = sb("reserve_rs", [P, PACK], F32)
+        nc.scalar.copy(reserve_sb[:], vectors_t[:, 0:PACK])
+        nc.scalar.copy(rs_sb[:], vectors_t[:, PACK : 2 * PACK])
+        nc.scalar.activation(minus_rs[:], vectors_t[:, PACK : 2 * PACK], ACT.Copy, scale=-1.0)
+        for t in range(PACK):
+            nc.scalar.activation(reserve_rs[:, t : t + 1], vectors_t[:, t : t + 1], ACT.Copy, scale=rs_sb[:, t : t + 1])
+
         h_first = [sb("h_first%d" % t, [P, M], F32) for t in range(PACK)]
         h_second = [sb("h_second%d" % t, [P, M], F32) for t in range(PACK)]
         own = [sb("own%d" % t, [P, M], F32) for t in range(PACK)]
@@ -154,7 +157,9 @@ def tile_attend_tratiopairs_o_pl_kernel(
             inv_t = sb("inv_t%d" % u, [P, PACK * P], F32)
             nc.scalar.activation(root_t[:], den_t[u][:].rearrange("p t r -> p (t r)"), ACT.Abs_reciprocal_sqrt)
             nc.scalar.activation(inv_t[:], root_t[:], ACT.Square)
-            nc.scalar.activation(inv_sq_t[u][:], inv_t[:].rearrange("p (w e r) -> p w r e", w=2, e=2), ACT.Square)
+            nc.scalar.activation(
+                inv_sq_t[u][:].rearrange("p w q e -> p q w e"), inv_t[:].rearrange("p (q w e) -> p q w e", w=2, e=2), ACT.Square
+            )
 
         th1 = [sb("th1_%d" % t, [P, J], F32) for t in range(PACK)]
         for t in range(PACK):
@@ -166,12 +171,6 @@ def tile_attend_tratiopairs_o_pl_kernel(
                 wor_bf[:, :, q * 32 : (q + 1) * 32, :].rearrange("p t m j -> p m j t"),
                 wor_raw[:, :, q * P : (q + 1) * P].rearrange("p j (m t) -> p m j t", t=PACK),
             )
-        wor_codes = sb("wor_codes", [P, F], U32)
-        wor_scales = sb("wor_scales", [P, F], U8)
-        nc.vector.quantize_mx(
-            out=wor_codes[:].bitcast(FP8X4), scales=wor_scales[:], in_=wor_bf[:].rearrange("p t m j -> p (t m j)")
-        )
-
         numer_t = [bank("numer_t%d" % u, HALVES + u, [P, PACK, P]) for u in range(HALVES)]
         for t in range(PACK):
             gain = sb("gain%d" % t, [P, M], F32)
@@ -185,13 +184,20 @@ def tile_attend_tratiopairs_o_pl_kernel(
                         numer_t[u][:, t, :], lhsT=term[:, cols], rhs=ident[:], is_transpose=True, start=(n == 0), stop=(n == 1)
                     )
 
-        y_bf = sb("y_bf", [P, M, PACK], BF16)
+        wor_codes = sb("th1_%d" % (PACK - 1), [P, F], U32)
+        wor_scales = sb("wor_scales", [P, F], U8)
+        nc.vector.quantize_mx(
+            out=wor_codes[:].bitcast(FP8X4), scales=wor_scales[:], in_=wor_bf[:].rearrange("p t m j -> p (t m j)")
+        )
+
+        y_codes = sb("y_codes", [P, M], U32)
+        y_scales = sb("y_scales", [P, M], U8)
         out_rows = out_0.rearrange("(p t) m -> p t m", t=PACK)
         fo_codes, fo_scales = [], []
         for u in range(HALVES):
             fo_t = sb("fo_t%d" % u, [P, 2, P, 2], BF16)
             nc.vector.tensor_tensor(
-                fo_t[:], numer_t[u][:].rearrange("p (w e) r -> p w r e", e=2), inv_sq_t[u][:], ALU.mult
+                fo_t[:], numer_t[u][:].rearrange("p t (s w e) -> p w (t s) e", w=2, e=2), inv_sq_t[u][:], ALU.mult
             )
             fo_words = fo_t[:].rearrange("p w r e -> p (w r e)").bitcast(F32)
             turned = bank("turned%d" % u, u, [P, 2, MH])
@@ -223,13 +229,12 @@ def tile_attend_tratiopairs_o_pl_kernel(
             y = sb("y%d" % u, [P, PACK, MH], F32)
             nc.vector.tensor_tensor(y[:], yo[:], res_sb[:, :, cols], ALU.add)
             nc.sync.dma_start(out_rows[:, :, cols], y[:])
-            nc.scalar.copy(
-                y_bf[:, cols, :].rearrange("p (a i) t -> p a t i", i=4), y[:].rearrange("p t (a i) -> p a t i", i=4)
+            y_bf = sb("y_bf%d" % u, [P, MH, PACK], BF16)
+            nc.scalar.copy(y_bf[:].rearrange("p (a i) t -> p a t i", i=4), y[:].rearrange("p t (a i) -> p a t i", i=4))
+            nc.vector.quantize_mx(
+                out=y_codes[:, cols].bitcast(FP8X4), scales=y_scales[:, cols], in_=y_bf[:].rearrange("p m t -> p (m t)")
             )
 
-        y_codes = sb("y_codes", [P, M], U32)
-        y_scales = sb("y_scales", [P, M], U8)
-        nc.vector.quantize_mx(out=y_codes[:].bitcast(FP8X4), scales=y_scales[:], in_=y_bf[:].rearrange("p m t -> p (m t)"))
         nc.sync.dma_start(out_1[0].rearrange("p m t -> p (m t)").bitcast(I32), y_codes[:].bitcast(I32))
         for q, queue in enumerate((nc.scalar, nc.sync, nc.scalar, nc.sync)):
             queue.dma_start(out_2[0, 4 * q : 4 * q + 4, :].bitcast(I32), y_scales[32 * q : 32 * q + 4, :].bitcast(I32))

@@ -21,6 +21,7 @@ PACK = 4
 QUADS = 4
 HALVES = 2
 MH = M // HALVES
+ON_GPSIMD = 2
 
 
 def tile_attend_tratiopairs_o_pl_kernel(
@@ -118,6 +119,11 @@ def tile_attend_tratiopairs_o_pl_kernel(
         ta = [bank("ta%d" % t, PACK + t, [P, J]) for t in range(PACK)]
         for t in range(PACK):
             first_layer(ta[t], t, dtab_gw, dtab_gs)
+        th1 = [sb("th1_%d" % t, [P, J], F32) for t in range(PACK)]
+        for t in range(ON_GPSIMD):
+            ta_sb = sb("ta_sb%d" % t, [P, J], F32)
+            nc.scalar.copy(ta_sb[:], ta[t][:])
+            nc.gpsimd.tensor_tensor(th1[t][:], ta_sb[:], h1[t][:], ALU.mult)
 
         vectors_t = bank("vectors_t", PACK - 1, [P, P])
         nc.tensor.transpose(vectors_t[:], vectors[:], ident[:])
@@ -161,8 +167,7 @@ def tile_attend_tratiopairs_o_pl_kernel(
                 inv_sq_t[u][:].rearrange("p w q e -> p q w e"), inv_t[:].rearrange("p (q w e) -> p q w e", w=2, e=2), ACT.Square
             )
 
-        th1 = [sb("th1_%d" % t, [P, J], F32) for t in range(PACK)]
-        for t in range(PACK):
+        for t in range(ON_GPSIMD, PACK):
             nc.vector.tensor_tensor(th1[t][:], ta[t][:], h1[t][:], ALU.mult)
 
         wor_bf = sb("wor_bf", [P, PACK, P, PACK], BF16)

@@ -21,7 +21,7 @@ PACK = 4
 QUADS = 4
 HALVES = 2
 MH = M // HALVES
-ON_GPSIMD = 2
+GPSIMD_COLUMNS = 1280
 
 
 def tile_attend_tratiopairs_o_pl_kernel(
@@ -69,11 +69,21 @@ def tile_attend_tratiopairs_o_pl_kernel(
         load_words(dtab_w, dtab_words)
         nc.sync.dma_start(firsts[:], offs2)
         nc.sync.dma_start(seconds[:], offs3)
-        nc.sync.dma_start(vectors[0:PACK, :], reserve.rearrange("(t p) o -> t (p o)", t=PACK))
-        nc.sync.dma_start(vectors[PACK : 2 * PACK, :], rs.rearrange("(t p) o -> t (p o)", t=PACK))
+        nc.gpsimd.dma_start(vectors[0:PACK, :], reserve.rearrange("(t p) o -> t (p o)", t=PACK))
+        nc.gpsimd.dma_start(vectors[PACK : 2 * PACK, :], rs.rearrange("(t p) o -> t (p o)", t=PACK))
 
         ident = sb("ident", [P, P], F32)
         make_identity(nc, ident[:])
+
+        vectors_t = bank("vectors_t", PACK, [P, P])
+        nc.tensor.transpose(vectors_t[:], vectors[:], ident[:])
+        columns = sb("columns", [P, 2 * PACK], F32)
+        nc.scalar.copy(columns[:], vectors_t[:, 0 : 2 * PACK])
+        reserve_sb, rs_sb = columns[:, 0:PACK], columns[:, PACK : 2 * PACK]
+        minus_rs = sb("minus_rs", [P, PACK], F32)
+        reserve_rs = sb("reserve_rs", [P, PACK], F32)
+        nc.gpsimd.tensor_scalar(minus_rs[:], rs_sb, -1.0, 0.0, ALU.mult, ALU.add)
+        nc.gpsimd.tensor_tensor(reserve_rs[:], reserve_sb, rs_sb, ALU.mult)
 
         tab_gw = sb("tab_gw", [P, J], U32)
         tab_gs = sb("tab_gs", [P, J], U8)
@@ -120,22 +130,12 @@ def tile_attend_tratiopairs_o_pl_kernel(
         for t in range(PACK):
             first_layer(ta[t], t, dtab_gw, dtab_gs)
         th1 = [sb("th1_%d" % t, [P, J], F32) for t in range(PACK)]
-        for t in range(ON_GPSIMD):
-            ta_sb = sb("ta_sb%d" % t, [P, J], F32)
-            nc.scalar.copy(ta_sb[:], ta[t][:])
-            nc.gpsimd.tensor_tensor(th1[t][:], ta_sb[:], h1[t][:], ALU.mult)
-
-        vectors_t = bank("vectors_t", PACK - 1, [P, P])
-        nc.tensor.transpose(vectors_t[:], vectors[:], ident[:])
-        reserve_sb = sb("reserve_sb", [P, PACK], F32)
-        rs_sb = sb("rs_sb", [P, PACK], F32)
-        minus_rs = sb("minus_rs", [P, PACK], F32)
-        reserve_rs = sb("reserve_rs", [P, PACK], F32)
-        nc.scalar.copy(reserve_sb[:], vectors_t[:, 0:PACK])
-        nc.scalar.copy(rs_sb[:], vectors_t[:, PACK : 2 * PACK])
-        nc.scalar.activation(minus_rs[:], vectors_t[:, PACK : 2 * PACK], ACT.Copy, scale=-1.0)
-        for t in range(PACK):
-            nc.scalar.activation(reserve_rs[:, t : t + 1], vectors_t[:, t : t + 1], ACT.Copy, scale=rs_sb[:, t : t + 1])
+        shares = [min(J, max(0, GPSIMD_COLUMNS - t * J)) for t in range(PACK)]
+        for t, share in enumerate(shares):
+            if share:
+                ta_sb = sb("ta_sb%d" % t, [P, share], F32)
+                nc.scalar.copy(ta_sb[:], ta[t][:, :share])
+                nc.gpsimd.tensor_tensor(th1[t][:, :share], ta_sb[:], h1[t][:, :share], ALU.mult)
 
         h_first = [sb("h_first%d" % t, [P, M], F32) for t in range(PACK)]
         h_second = [sb("h_second%d" % t, [P, M], F32) for t in range(PACK)]
@@ -167,8 +167,9 @@ def tile_attend_tratiopairs_o_pl_kernel(
                 inv_sq_t[u][:].rearrange("p w q e -> p q w e"), inv_t[:].rearrange("p (q w e) -> p q w e", w=2, e=2), ACT.Square
             )
 
-        for t in range(ON_GPSIMD, PACK):
-            nc.vector.tensor_tensor(th1[t][:], ta[t][:], h1[t][:], ALU.mult)
+        for t, share in reversed(list(enumerate(shares))):
+            if share < J:
+                nc.vector.tensor_tensor(th1[t][:, share:], ta[t][:, share:], h1[t][:, share:], ALU.mult)
 
         wor_bf = sb("wor_bf", [P, PACK, P, PACK], BF16)
         for q in range(4):
@@ -180,8 +181,12 @@ def tile_attend_tratiopairs_o_pl_kernel(
         for t in range(PACK):
             gain = sb("gain%d" % t, [P, M], F32)
             loss = sb("loss%d" % t, [P, M], F32)
-            nc.vector.tensor_tensor(gain[:], th1[t][:].indirect(firsts[:]), rest[t][:], ALU.mult)
-            nc.vector.tensor_tensor(loss[:], th1[t][:].indirect(seconds[:]), own[t][:], ALU.mult)
+            pieces = HALVES if t == PACK - 1 else 1
+            for piece in range(pieces):
+                cols = slice(piece * M // pieces, (piece + 1) * M // pieces)
+                entries = slice(cols.start // 16, cols.stop // 16)
+                nc.vector.tensor_tensor(gain[:, cols], th1[t][:].indirect(firsts[:, entries]), rest[t][:, cols], ALU.mult)
+                nc.vector.tensor_tensor(loss[:, cols], th1[t][:].indirect(seconds[:, entries]), own[t][:, cols], ALU.mult)
             for u in range(HALVES):
                 cols = slice(u * MH, (u + 1) * MH)
                 for n, term in enumerate((gain, loss)):
@@ -189,12 +194,7 @@ def tile_attend_tratiopairs_o_pl_kernel(
                         numer_t[u][:, t, :], lhsT=term[:, cols], rhs=ident[:], is_transpose=True, start=(n == 0), stop=(n == 1)
                     )
 
-        wor_codes = sb("th1_%d" % (PACK - 1), [P, F], U32)
-        wor_scales = sb("wor_scales", [P, F], U8)
-        nc.vector.quantize_mx(
-            out=wor_codes[:].bitcast(FP8X4), scales=wor_scales[:], in_=wor_bf[:].rearrange("p t m j -> p (t m j)")
-        )
-
+        y_bf = sb("y_bf", [P, M, PACK], BF16)
         y_codes = sb("y_codes", [P, M], U32)
         y_scales = sb("y_scales", [P, M], U8)
         out_rows = out_0.rearrange("(p t) m -> p t m", t=PACK)
@@ -218,28 +218,38 @@ def tile_attend_tratiopairs_o_pl_kernel(
             nc.vector.quantize_mx(
                 out=fo_codes[u][:].bitcast(FP8X4), scales=fo_scales[u][:], in_=fo_bf[:].rearrange("p m t -> p (m t)")
             )
+        wor_codes = sb("inv_sq_t%d" % (HALVES - 1), [P, F], U32)
+        wor_scales = sb("wor_scales", [P, F], U8)
+        nc.vector.quantize_mx(
+            out=wor_codes[:].bitcast(FP8X4), scales=wor_scales[:], in_=wor_bf[:].rearrange("p t m j -> p (t m j)")
+        )
         for u in range(HALVES):
             cols = slice(u * MH, (u + 1) * MH)
-            yo = bank("yo%d" % u, PACK + u, [P, PACK, MH])
-            for t in range(PACK):
-                nc.tensor.matmul_mx(
-                    out=yo[:, t, :],
-                    lhsT=wor_codes[:, t * P : (t + 1) * P].bitcast(FP8X4),
-                    lhsT_scale=wor_scales[:, t * P : (t + 1) * P],
-                    rhs=fo_codes[u][:].bitcast(FP8X4),
-                    rhs_scale=fo_scales[u][:],
-                    start=True,
-                    stop=True,
-                )
             y = sb("y%d" % u, [P, PACK, MH], F32)
-            nc.vector.tensor_tensor(y[:], yo[:], res_sb[:, :, cols], ALU.add)
+            for pair in range(2):
+                yo = bank("yo%d_%d" % (u, pair), PACK + 2 * u + pair, [P, 2, MH])
+                for e in range(2):
+                    t = 2 * pair + e
+                    nc.tensor.matmul_mx(
+                        out=yo[:, e, :],
+                        lhsT=wor_codes[:, t * P : (t + 1) * P].bitcast(FP8X4),
+                        lhsT_scale=wor_scales[:, t * P : (t + 1) * P],
+                        rhs=fo_codes[u][:].bitcast(FP8X4),
+                        rhs_scale=fo_scales[u][:],
+                        start=True,
+                        stop=True,
+                    )
+                rows = slice(2 * pair, 2 * pair + 2)
+                nc.vector.tensor_tensor(y[:, rows, :], yo[:], res_sb[:, rows, cols], ALU.add)
             nc.sync.dma_start(out_rows[:, :, cols], y[:])
-            y_bf = sb("y_bf%d" % u, [P, MH, PACK], BF16)
-            nc.scalar.copy(y_bf[:].rearrange("p (a i) t -> p a t i", i=4), y[:].rearrange("p t (a i) -> p a t i", i=4))
-            nc.vector.quantize_mx(
-                out=y_codes[:, cols].bitcast(FP8X4), scales=y_scales[:, cols], in_=y_bf[:].rearrange("p m t -> p (m t)")
-            )
-
+            woven = y_bf[:, cols, :].rearrange("p (a i) t -> p a t i", i=4)
+            planar = y[:].rearrange("p t (a i) -> p a t i", i=4)
+            if u < HALVES - 1:
+                nc.scalar.copy(woven, planar)
+            else:
+                nc.scalar.copy(woven[:, :12], planar[:, :12])
+                nc.vector.tensor_copy(woven[:, 12:], planar[:, 12:])
+        nc.vector.quantize_mx(out=y_codes[:].bitcast(FP8X4), scales=y_scales[:], in_=y_bf[:].rearrange("p m t -> p (m t)"))
         nc.sync.dma_start(out_1[0].rearrange("p m t -> p (m t)").bitcast(I32), y_codes[:].bitcast(I32))
         for q, queue in enumerate((nc.scalar, nc.sync, nc.scalar, nc.sync)):
             queue.dma_start(out_2[0, 4 * q : 4 * q + 4, :].bitcast(I32), y_scales[32 * q : 32 * q + 4, :].bitcast(I32))

from contextlib import ExitStack

import concourse.mybir as mybir
from concourse.masks import make_identity

K, R, F, T, J, M = 512, 512, 512, 2048, 512, 256
FLOPS = 2 * K * R * J * 2 + 2 * R * F * M

F32 = mybir.dt.float32
BF16 = mybir.dt.bfloat16
I32 = mybir.dt.int32
U32 = mybir.dt.uint32
U16 = mybir.dt.uint16
U8 = mybir.dt.uint8
FP8X4 = mybir.dt.float8_e4m3fn_x4
ACT = mybir.ActivationFunctionType
ALU = mybir.AluOpType

P = 128
PACK = 4
QUADS = 4
HALVES = 2
MH = M // HALVES
GPSIMD_COLUMNS = 1280


def tile_attend_tratiopairs_o_pl_kernel(
    tc, dtab_words, dtab_scales, tab_words, tab_scales, w1, reserve, rs, wor, res, offs, offs2, offs3, out_0, out_1, out_2
):
    nc = tc.nc
    with ExitStack() as ctx:
        keep = ctx.enter_context(tc.tile_pool(name="keep", bufs=1))
        psum = ctx.enter_context(tc.psum_pool(name="psum", bufs=1))

        def sb(name, shape, dtype):
            return keep.tile(shape, dtype, name=name, align_bytes=64)

        def bank(name, number, shape):
            return psum.tile(shape, F32, name=name, tag="bank%d" % number)

        def load_scale_rows(queues, plane, rows):
            for i, queue in enumerate(queues):
                queue.dma_start(plane[i:P:32, :].bitcast(I32), rows[0, i:16:4, :].bitcast(I32))

        def load_words(tile, words):
            nc.sync.dma_start(tile[:].bitcast(I32), words[0].rearrange("p n t -> p (n t)").bitcast(I32))

        slots = sb("slots", [P, J // 16], U16)
        firsts = sb("firsts", [P, M // 16], U16)
        seconds = sb("seconds", [P, M // 16], U16)
        tab_w = sb("tab_w", [P, T], U32)
        dtab_w = sb("dtab_w", [P, T], U32)
        tab_s = sb("tab_s", [P, T], U8)
        dtab_s = sb("dtab_s", [P, T], U8)
        w1_raw = [sb("w1_raw%d" % h, [P, PACK, R // 2], F32) for h in range(2)]
        vectors = sb("vectors", [P, P], F32)

        nc.gpsimd.memset(tab_s[:].bitcast(I32), 0)
        nc.gpsimd.memset(dtab_s[:].bitcast(I32), 0)
        nc.gpsimd.memset(vectors[:], 0.0)

        nc.sync.dma_start(slots[:], offs)
        load_words(tab_w, tab_words)
        load_scale_rows((nc.sync,) * 4, tab_s, tab_scales)
        w1_rows = w1.rearrange("(p j) c -> p j c", j=PACK)
        for h in range(2):
            nc.sync.dma_start(w1_raw[h][:], w1_rows[:, :, h * (R // 2) : (h + 1) * (R // 2)])
        load_scale_rows((nc.sync,) * 4, dtab_s, dtab_scales)
        load_words(dtab_w, dtab_words)
        nc.sync.dma_start(firsts[:], offs2)
        nc.sync.dma_start(seconds[:], offs3)
        nc.gpsimd.dma_start(vectors[0:PACK, :], reserve.rearrange("(t p) o -> t (p o)", t=PACK))
        nc.gpsimd.dma_start(vectors[PACK : 2 * PACK, :], rs.rearrange("(t p) o -> t (p o)", t=PACK))

        ident = sb("ident", [P, P], F32)
        make_identity(nc, ident[:])

        vectors_t = bank("vectors_t", PACK, [P, P])
        nc.tensor.transpose(vectors_t[:], vectors[:], ident[:])
        columns = sb("columns", [P, 2 * PACK], F32)
        nc.scalar.copy(columns[:], vectors_t[:, 0 : 2 * PACK])
        reserve_sb, rs_sb = columns[:, 0:PACK], columns[:, PACK : 2 * PACK]
        minus_rs = sb("minus_rs", [P, PACK], F32)
        reserve_rs = sb("reserve_rs", [P, PACK], F32)
        nc.gpsimd.tensor_scalar(minus_rs[:], rs_sb, -1.0, 0.0, ALU.mult, ALU.add)
        nc.gpsimd.tensor_tensor(reserve_rs[:], reserve_sb, rs_sb, ALU.mult)

        tab_gw = sb("tab_gw", [P, J], U32)
        tab_gs = sb("tab_gs", [P, J], U8)
        dtab_gw = sb("dtab_gw", [P, J], U32)
        dtab_gs = sb("dtab_gs", [P, J], U8)
        nc.vector.tensor_copy(tab_gw[:], tab_w[:].indirect(slots[:]))
        nc.vector.tensor_copy(tab_gs[:], tab_s[:].indirect(slots[:]))

        w1_bf = [sb("w1_bf%d" % h, [P, R // 2, PACK], BF16) for h in range(2)]
        w1_codes = [sb("w1_codes%d" % h, [P, 2 * P], U32) for h in range(2)]
        w1_scales = [sb("w1_scales%d" % h, [P, 2 * P], U8) for h in range(2)]
        for h in range(2):
            nc.scalar.activation(
                w1_bf[h][:].rearrange("p (a i) j -> p a j i", i=4), w1_raw[h][:].rearrange("p j (a i) -> p a j i", i=4), ACT.Copy
            )
            nc.vector.quantize_mx(
                out=w1_codes[h][:].bitcast(FP8X4), scales=w1_scales[h][:], in_=w1_bf[h][:].rearrange("p c j -> p (c j)")
            )
        nc.vector.tensor_copy(dtab_gs[:], dtab_s[:].indirect(slots[:]))
        nc.vector.tensor_copy(dtab_gw[:], dtab_w[:].indirect(slots[:]))

        wor_raw = sb("tab_w", [P, PACK, F], F32)
        nc.sync.dma_start(wor_raw[:], wor.rearrange("(p j) c -> p j c", j=PACK))
        res_sb = sb("w1_raw0", [P, PACK, M], F32)
        nc.sync.dma_start(res_sb[:], res.rearrange("(p t) m -> p t m", t=PACK))

        def first_layer(acc, t, words, scales):
            nc.tensor.matmul_mx(
                out=acc[:],
                lhsT=w1_codes[t // 2][:, (t % 2) * P : (t % 2 + 1) * P].bitcast(FP8X4),
                lhsT_scale=w1_scales[t // 2][:, (t % 2) * P : (t % 2 + 1) * P],
                rhs=words[:].bitcast(FP8X4),
                rhs_scale=scales[:],
                start=True,
                stop=True,
            )

        h1 = [sb("h1_%d" % t, [P, J], F32) for t in range(PACK)]
        for t in range(PACK):
            a = bank("a%d" % t, t, [P, J])
            first_layer(a, t, tab_gw, tab_gs)
            nc.scalar.activation(h1[t][:], a[:], ACT.Exp)
        ta = [bank("ta%d" % t, PACK + t, [P, J]) for t in range(PACK)]
        for t in range(PACK):
            first_layer(ta[t], t, dtab_gw, dtab_gs)
        th1 = [sb("th1_%d" % t, [P, J], F32) for t in range(PACK)]
        shares = [min(J, max(0, GPSIMD_COLUMNS - t * J)) for t in range(PACK)]
        for t, share in enumerate(shares):
            if share:
                ta_sb = sb("ta_sb%d" % t, [P, share], F32)
                nc.scalar.copy(ta_sb[:], ta[t][:, :share])
                nc.gpsimd.tensor_tensor(th1[t][:, :share], ta_sb[:], h1[t][:, :share], ALU.mult)

        h_first = [sb("h_first%d" % t, [P, M], F32) for t in range(PACK)]
        h_second = [sb("h_second%d" % t, [P, M], F32) for t in range(PACK)]
        own = [sb("own%d" % t, [P, M], F32) for t in range(PACK)]
        rest = [sb("rest%d" % t, [P, M], F32) for t in range(PACK)]
        den_t = [bank("den_t%d" % u, u, [P, PACK, P]) for u in range(HALVES)]
        for t in range(PACK):
            nc.vector.tensor_copy(h_first[t][:], h1[t][:].indirect(firsts[:]))
            nc.vector.tensor_copy(h_second[t][:], h1[t][:].indirect(seconds[:]))
            for u in range(HALVES):
                cols = slice(u * MH, (u + 1) * MH)
                terms = (reserve_sb[:, t : t + 1].to_broadcast([P, P]), h_first[t][:, cols], h_second[t][:, cols])
                for n, term in enumerate(terms):
                    nc.tensor.matmul(
                        den_t[u][:, t, :], lhsT=term, rhs=ident[:], is_transpose=True, start=(n == 0), stop=(n == len(terms) - 1)
                    )
            nc.scalar.activation(own[t][:], h_first[t][:], ACT.Copy, scale=minus_rs[:, t : t + 1])
            nc.scalar.activation(
                rest[t][:], h_second[t][:], ACT.Identity, scale=rs_sb[:, t : t + 1], bias=reserve_rs[:, t : t + 1]
            )

        inv_sq_t = [sb("inv_sq_t%d" % u, [P, 2, P, 2], F32) for u in range(HALVES)]
        for u in range(HALVES):
            root_t = sb("root_t%d" % u, [P, PACK * P], F32)
            inv_t = sb("inv_t%d" % u, [P, PACK * P], F32)
            nc.scalar.activation(root_t[:], den_t[u][:].rearrange("p t r -> p (t r)"), ACT.Abs_reciprocal_sqrt)
            nc.scalar.activation(inv_t[:], root_t[:], ACT.Square)
            nc.scalar.activation(
                inv_sq_t[u][:].rearrange("p w q e -> p q w e"), inv_t[:].rearrange("p (q w e) -> p q w e", w=2, e=2), ACT.Square
            )

        for t, share in reversed(list(enumerate(shares))):
            if share < J:
                nc.vector.tensor_tensor(th1[t][:, share:], ta[t][:, share:], h1[t][:, share:], ALU.mult)

        wor_bf = sb("wor_bf", [P, PACK, P, PACK], BF16)
        for q in range(4):
            nc.scalar.copy(
                wor_bf[:, :, q * 32 : (q + 1) * 32, :].rearrange("p t m j -> p m j t"),
                wor_raw[:, :, q * P : (q + 1) * P].rearrange("p j (m t) -> p m j t", t=PACK),
            )
        numer_t = [bank("numer_t%d" % u, HALVES + u, [P, PACK, P]) for u in range(HALVES)]
        for t in range(PACK):
            gain = sb("gain%d" % t, [P, M], F32)
            loss = sb("loss%d" % t, [P, M], F32)
            pieces = HALVES if t == PACK - 1 else 1
            for piece in range(pieces):
                cols = slice(piece * M // pieces, (piece + 1) * M // pieces)
                entries = slice(cols.start // 16, cols.stop // 16)
                nc.vector.tensor_tensor(gain[:, cols], th1[t][:].indirect(firsts[:, entries]), rest[t][:, cols], ALU.mult)
                nc.vector.tensor_tensor(loss[:, cols], th1[t][:].indirect(seconds[:, entries]), own[t][:, cols], ALU.mult)
            for u in range(HALVES):
                cols = slice(u * MH, (u + 1) * MH)
                for n, term in enumerate((gain, loss)):
                    nc.tensor.matmul(
                        numer_t[u][:, t, :], lhsT=term[:, cols], rhs=ident[:], is_transpose=True, start=(n == 0), stop=(n == 1)
                    )

        y_bf = sb("y_bf", [P, M, PACK], BF16)
        y_codes = sb("y_codes", [P, M], U32)
        y_scales = sb("y_scales", [P, M], U8)
        out_rows = out_0.rearrange("(p t) m -> p t m", t=PACK)
        fo_codes, fo_scales = [], []
        for u in range(HALVES):
            fo_t = sb("fo_t%d" % u, [P, 2, P, 2], BF16)
            nc.vector.tensor_tensor(
                fo_t[:], numer_t[u][:].rearrange("p t (s w e) -> p w (t s) e", w=2, e=2), inv_sq_t[u][:], ALU.mult
            )
            fo_words = fo_t[:].rearrange("p w r e -> p (w r e)").bitcast(F32)
            turned = bank("turned%d" % u, u, [P, 2, MH])
            for w in range(2):
                nc.tensor.transpose(turned[:, w, :], fo_words[:, w * P : (w + 1) * P], ident[:])
            fo_bf = sb("fo_bf%d" % u, [P, MH, PACK], BF16)
            nc.scalar.copy(
                fo_bf[:].rearrange("p m t -> p (m t)").bitcast(F32).rearrange("p (m w) -> p m w", w=2),
                turned[:].rearrange("p w m -> p m w"),
            )
            fo_codes.append(sb("fo_codes%d" % u, [P, MH], U32))
            fo_scales.append(sb("fo_scales%d" % u, [P, MH], U8))
            nc.vector.quantize_mx(
                out=fo_codes[u][:].bitcast(FP8X4), scales=fo_scales[u][:], in_=fo_bf[:].rearrange("p m t -> p (m t)")
            )
        wor_codes = sb("inv_sq_t%d" % (HALVES - 1), [P, F], U32)
        wor_scales = sb("wor_scales", [P, F], U8)
        nc.vector.quantize_mx(
            out=wor_codes[:].bitcast(FP8X4), scales=wor_scales[:], in_=wor_bf[:].rearrange("p t m j -> p (t m j)")
        )
        for u in range(HALVES):
            cols = slice(u * MH, (u + 1) * MH)
            y = sb("y%d" % u, [P, PACK, MH], F32)
            for pair in range(2):
                yo = bank("yo%d_%d" % (u, pair), PACK + 2 * u + pair, [P, 2, MH])
                for e in range(2):
                    t = 2 * pair + e
                    nc.tensor.matmul_mx(
                        out=yo[:, e, :],
                        lhsT=wor_codes[:, t * P : (t + 1) * P].bitcast(FP8X4),
                        lhsT_scale=wor_scales[:, t * P : (t + 1) * P],
                        rhs=fo_codes[u][:].bitcast(FP8X4),
                        rhs_scale=fo_scales[u][:],
                        start=True,
                        stop=True,
                    )
                rows = slice(2 * pair, 2 * pair + 2)
                nc.vector.tensor_tensor(y[:, rows, :], yo[:], res_sb[:, rows, cols], ALU.add)
            nc.sync.dma_start(out_rows[:, :, cols], y[:])
            woven = y_bf[:, cols, :].rearrange("p (a i) t -> p a t i", i=4)
            planar = y[:].rearrange("p t (a i) -> p a t i", i=4)
            if u < HALVES - 1:
                nc.scalar.copy(woven, planar)
            else:
                nc.scalar.copy(woven[:, :12], planar[:, :12])
                nc.vector.tensor_copy(woven[:, 12:], planar[:, 12:])
        nc.vector.quantize_mx(out=y_codes[:].bitcast(FP8X4), scales=y_scales[:], in_=y_bf[:].rearrange("p m t -> p (m t)"))
        nc.sync.dma_start(out_1[0].rearrange("p m t -> p (m t)").bitcast(I32), y_codes[:].bitcast(I32))
        for q, queue in enumerate((nc.scalar, nc.sync, nc.scalar, nc.sync)):
            queue.dma_start(out_2[0, 4 * q : 4 * q + 4, :].bitcast(I32), y_scales[32 * q : 32 * q + 4, :].bitcast(I32))
